import numpy as np
import ml_dtypes


def mxq(x, axis, fmt="e4m3"):
    dtype, down = {"e4m3": (ml_dtypes.float8_e4m3fn, 7), "e5m2": (ml_dtypes.float8_e5m2, 14)}[fmt]
    v = np.moveaxis(np.asarray(x, np.float32).astype(ml_dtypes.bfloat16).astype(np.float64), axis, -1)
    blocks = v.reshape(v.shape[:-1] + (-1, 32))
    amax = np.abs(blocks).max(-1, keepdims=True)
    byte = np.maximum(np.where(amax > 0, np.frexp(amax)[1] - 1 + 127, 0) - down, 1)
    scale = np.exp2(byte - 127.0)
    codes = (blocks / scale).astype(np.float32).astype(dtype).astype(np.float64)
    return np.moveaxis((codes * scale).reshape(v.shape), -1, axis)


WIDE = False


def mx_kscale(k, group=512):
    if not WIDE:
        return np.ones(k)
    levels = np.array([18, -18])
    if group != 512:
        return np.exp2(np.random.permutation(np.resize(levels, k // group))).repeat(group)
    if k % 512:
        return np.exp2(np.random.permutation(np.resize(levels, k // 32))).repeat(32)
    a = np.empty((k // 512, 16))
    for p in range(k // 512):
        a[p, :8] = np.random.permutation(np.resize(levels, 8))
        for g in range(8):
            far = levels[np.abs(levels - a[p, g]) >= 10]
            a[p, g + 8] = far[np.random.randint(len(far))]
    return np.exp2(a.ravel()).repeat(32)


def f64(x):
    return np.asarray(x).astype(np.float64)


G, D, M, O, N = 4, 128, 128, 128, 512


def setup_inputs():
    n = np.random.standard_normal
    s_d = mx_kscale(D, 0)
    s_o = mx_kscale(O, 0)
    return {
        "x": (n((G, D, N)) * s_d[:, None]).astype(np.float32),
        "w1": (n((G, D, M)) / np.sqrt(D) / s_d[:, None]).astype(np.float32),
        "w2": (n((G, D, M)) / np.sqrt(D) / s_d[:, None]).astype(np.float32),
        "ra": (np.random.uniform(0.3, 1.5, (G, M, 1))).astype(np.float32),
        "wo": (n((G, O, M)) / np.sqrt(O) / s_o[:, None]).astype(np.float32),
        "dy": (n((G, O, N)) * s_o[:, None]).astype(np.float32),
        "old": (0.3 * n((G, M, N))).astype(np.float32),
    }


def reference(x, w1, w2, ra, wo, dy, old):
    w1q = mxq(f64(w1), 1, "e4m3")
    xq = mxq(f64(x), 1, "e4m3")
    z1 = w1q.transpose(0, 2, 1) @ xq
    w2q = mxq(f64(w2), 1, "e4m3")
    z2 = w2q.transpose(0, 2, 1) @ xq
    nn = np.sqrt(np.square(z1) + np.square(z2) + f64(ra))
    woq = mxq(f64(wo), 1, "e4m3")
    dyq = mxq(f64(dy), 1, "e4m3")
    c0 = woq.transpose(0, 2, 1) @ dyq
    dnn = c0 * z1 / np.square(nn) * (-1.0)
    dz1 = c0 / nn + dnn * 0.5 / np.sqrt(np.square(z1) + np.square(z2) + f64(ra)) * z1 * 2.0
    y = dz1 + f64(old)
    return y

@@ -1,0 +1,230 @@
+from contextlib import ExitStack
+
+import concourse.mybir as mybir
+
+G, D, M, N = 4, 128, 128, 512
+FLOPS = 3 * 2 * G * D * M * N
+
+F32 = mybir.dt.float32
+BF16 = mybir.dt.bfloat16
+U32 = mybir.dt.uint32
+U8 = mybir.dt.uint8
+FP8X4 = mybir.dt.float8_e4m3fn_x4
+ACT = mybir.ActivationFunctionType
+ALU = mybir.AluOpType
+
+P = 128
+PACK = 4
+ROWS = D // PACK
+N_CALL = 128
+RUN = 4
+W = 128
+UNITS = N // W
+
+
+def tile_rows_bsphere_kernel(tc, x, w1, w2, ra, wo, dy, old, out):
+    nc = tc.nc
+    cols = [slice(W * c, W * (c + 1)) for c in range(UNITS)]
+
+    with ExitStack() as ctx:
+        sb = ctx.enter_context(tc.tile_pool(name="sb", bufs=1))
+        ps = ctx.enter_context(tc.psum_pool(name="ps", bufs=1))
+        ctx.enter_context(tc.manual_schedule())
+
+        z_bank = [ps.tile([P, N], F32, name="z%d" % g) for g in range(G)]
+        c_bank = [ps.tile([P, N], F32, name="c%d" % g) for g in range(G)]
+
+        def load_operand(name, src, first, count):
+            raw = sb.tile([P, PACK, count * W], F32, name="%s%d_raw" % (name, first))
+            nc.sync.dma_start(
+                out=raw[:],
+                in_=src[:, :, first * W : (first + count) * W].rearrange("g (p j) n -> (g p) j n", j=PACK),
+            )
+            return [
+                {
+                    "raw": raw[:, :, cols[u]],
+                    "bf": sb.tile([P, W, PACK], BF16, name="%s%d_bf" % (name, first + u), align_bytes=64),
+                    "codes": sb.tile([P, W], U32, name="%s%d_codes" % (name, first + u), align_bytes=64),
+                    "scales": sb.tile([P, W], U8, name="%s%d_scales" % (name, first + u), align_bytes=64),
+                }
+                for u in range(count)
+            ]
+
+        def load_old(first, count):
+            raw = sb.tile([P, G, count * W], F32, name="old%d" % first)
+            nc.sync.dma_start(out=raw[:], in_=old[:, :, first * W : (first + count) * W].rearrange("g m n -> m g n"))
+            return [raw[:, :, cols[u]] for u in range(count)]
+
+        def interleave(copy, op, n=slice(0, W)):
+            copy(
+                out=op["bf"][:, n, :].rearrange("p (c i) j -> p c j i", i=RUN),
+                in_=op["raw"][:, :, n].rearrange("p j (c i) -> p c j i", i=RUN),
+            )
+
+        def quantize(op):
+            nc.vector.quantize_mx(
+                out=op["codes"][:].bitcast(FP8X4),
+                scales=op["scales"][:],
+                in_=op["bf"][:].rearrange("p n j -> p (n j)"),
+            )
+
+        def product(target, weights, moving, g):
+            rows = slice(ROWS * g, ROWS * (g + 1))
+            nc.tensor.matmul_mx(
+                out=target,
+                lhsT=weights["codes"][rows, :].bitcast(FP8X4),
+                lhsT_scale=weights["scales"][rows, :],
+                rhs=moving["codes"][rows, :].bitcast(FP8X4),
+                rhs_scale=moving["scales"][rows, :],
+                start=True,
+                stop=True,
+            )
+
+        on_vector, on_scalar = nc.vector.tensor_copy, nc.scalar.copy
+
+        ra_rows = sb.tile([P, P], F32, name="ra_rows", align_bytes=64)
+        ra_cols = sb.tile([P, P], F32, name="ra_cols", align_bytes=64)
+        one = sb.tile([P, 8], F32, name="one")
+        warm = sb.tile([P, 8], F32, name="warm")
+        nc.vector.memset(ra_rows[:], 0.0)
+        nc.vector.memset(one[:], 1.0)
+        nc.scalar.dma_start(
+            out=ra_rows[0:P:32, :].rearrange("a (g i) -> a g i", g=G),
+            in_=ra.rearrange("g (a i) o -> a g (i o)", i=32),
+        )
+        nc.scalar.activation(out=warm[:], in_=one[:], func=ACT.Abs_reciprocal_sqrt)
+        ra_col = [ra_cols[:, 32 * g : 32 * g + 1] for g in range(G)]
+
+        xs = load_operand("x", x, 0, 1)
+        (w1q,) = load_operand("w1", w1, 0, 1)
+        (w2q,) = load_operand("w2", w2, 0, 1)
+        xs = xs + load_operand("x", x, 1, 1)
+        (woq,) = load_operand("wo", wo, 0, 1)
+        dys = load_operand("dy", dy, 0, 1)
+        xs = xs + load_operand("x", x, 2, 1)
+        dys = dys + load_operand("dy", dy, 1, 1)
+        olds = load_old(0, 1)
+        xs = xs + load_operand("x", x, 3, 1)
+        dys = dys + load_operand("dy", dy, 2, 2)
+        olds = olds + load_old(1, 3)
+
+        def planes(name, per=1):
+            return [sb.tile([P, G, per * W], F32, name="%s%d" % (name, c)) for c in range(UNITS)]
+
+        sq, s, r, r2, t, q, y, o = planes("sq", 2), planes("s"), planes("r"), planes("rr"), planes("t"), planes("q"), planes("y"), planes("o")
+        lo, hi, both = slice(0, 2), slice(2, 4), slice(0, 4)
+
+        def z_products(c):
+            for g in range(G):
+                product(z_bank[g][:, :W], w1q, xs[c], g)
+                product(z_bank[g][:, W : 2 * W], w2q, xs[c], g)
+
+        def c_products(c):
+            for g in range(G):
+                product(c_bank[g][:, cols[c]], woq, dys[c], g)
+
+        def squares(c, gs=both):
+            for g in range(gs.start, gs.stop):
+                nc.scalar.activation(out=sq[c][:, g, :], in_=z_bank[g][:, : 2 * W], func=ACT.Square)
+
+        def sums(c, gs=both):
+            nc.vector.tensor_tensor(out=s[c][:, gs, :], in0=sq[c][:, gs, :W], in1=sq[c][:, gs, W:], op=ALU.add)
+
+        def roots(c, gs=both):
+            for g in range(gs.start, gs.stop):
+                nc.scalar.activation(out=r[c][:, g, :], in_=s[c][:, g, :], func=ACT.Abs_reciprocal_sqrt, bias=ra_col[g])
+
+        def inverses(c, gs=both):
+            nc.scalar.activation(out=r2[c][:, gs, :], in_=r[c][:, gs, :], func=ACT.Square)
+
+        def numerators(c, gs=both):
+            for g in range(gs.start, gs.stop):
+                nc.vector.scalar_tensor_tensor(
+                    out=t[c][:, g, :], in0=sq[c][:, g, W:], scalar=ra_col[g], in1=c_bank[g][:, cols[c]],
+                    op0=ALU.add, op1=ALU.mult,
+                )
+
+        def by_root(c, gs=both):
+            nc.vector.tensor_tensor(out=q[c][:, gs, :], in0=t[c][:, gs, :], in1=r[c][:, gs, :], op=ALU.mult)
+
+        def by_inverse(c, gs=both):
+            nc.vector.tensor_tensor(out=y[c][:, gs, :], in0=q[c][:, gs, :], in1=r2[c][:, gs, :], op=ALU.mult)
+
+        def add_old(c, gs=both):
+            nc.vector.tensor_tensor(out=o[c][:, gs, :], in0=y[c][:, gs, :], in1=olds[c][:, gs, :], op=ALU.add)
+
+        def store(c, gs=both):
+            nc.sync.dma_start(out=out[gs, :, cols[c]].rearrange("g m n -> m g n"), in_=o[c][:, gs, :])
+
+        interleave(on_vector, xs[0])
+        interleave(on_vector, w1q)
+        quantize(xs[0])
+        interleave(on_scalar, w2q, slice(80, 128))
+        interleave(on_vector, w2q, slice(0, 80))
+        quantize(w1q)
+        for g in range(G):
+            product(c_bank[g][:, :W], w1q, xs[0], g)
+        quantize(w2q)
+        for g in range(G):
+            product(z_bank[g][:, :W], w2q, xs[0], g)
+        for g in range(G):
+            nc.scalar.activation(out=sq[0][:, g, :W], in_=c_bank[g][:, :W], func=ACT.Square)
+        for g in range(G):
+            nc.scalar.activation(out=sq[0][:, g, W:], in_=z_bank[g][:, :W], func=ACT.Square)
+        interleave(on_vector, xs[1])
+        nc.vector.transpose(out=ra_cols[:], in_=ra_rows[:])
+        quantize(xs[1])
+        z_products(1)
+        squares(1)
+        interleave(on_vector, woq)
+        quantize(woq)
+        interleave(on_vector, dys[0])
+        sums(0, lo)
+        quantize(dys[0])
+        c_products(0)
+        sums(0, hi)
+
+        interleave(on_vector, xs[2])
+        for c in range(UNITS):
+            first, last = c == 0, c + 1 == UNITS
+            roots(c)
+            if not last:
+                interleave(on_scalar, dys[c + 1])
+            if last:
+                inverses(c, lo)
+                inverses(c, hi)
+            else:
+                inverses(c)
+            if c + 3 < UNITS:
+                interleave(on_scalar, xs[c + 3])
+            numerators(c, lo)
+            if first:
+                quantize(xs[2])
+                z_products(2)
+            numerators(c, hi)
+            if c + 2 < UNITS:
+                squares(c + 2)
+            if first:
+                sums(1)
+            else:
+                add_old(c - 1)
+                store(c - 1)
+            if not last:
+                by_root(c)
+                quantize(dys[c + 1])
+                c_products(c + 1)
+                if not first:
+                    sums(c + 1)
+                by_inverse(c)
+                if first:
+                    quantize(xs[3])
+                    z_products(3)
+        c = UNITS - 1
+        by_root(c, lo)
+        by_root(c, hi)
+        by_inverse(c, lo)
+        by_inverse(c, hi)
+        add_old(c, lo)
+        store(c, lo)
+        add_old(c, hi)
+        store(c, hi)

@@ -18,8 +18,9 @@ PACK = 4
 ROWS = D // PACK
 N_CALL = 128
 RUN = 4
-W = 128
+W = 256
 UNITS = N // W
+XS = 128
 
 
 def tile_rows_bsphere_kernel(tc, x, w1, w2, ra, wo, dy, old, out):
@@ -34,51 +35,48 @@ def tile_rows_bsphere_kernel(tc, x, w1, w2, ra, wo, dy, old, out):
         z_bank = [ps.tile([P, N], F32, name="z%d" % g) for g in range(G)]
         c_bank = [ps.tile([P, N], F32, name="c%d" % g) for g in range(G)]
 
-        def load_operand(name, src, first, count):
-            raw = sb.tile([P, PACK, count * W], F32, name="%s%d_raw" % (name, first))
-            nc.sync.dma_start(
-                out=raw[:],
-                in_=src[:, :, first * W : (first + count) * W].rearrange("g (p j) n -> (g p) j n", j=PACK),
-            )
-            return [
-                {
-                    "raw": raw[:, :, cols[u]],
-                    "bf": sb.tile([P, W, PACK], BF16, name="%s%d_bf" % (name, first + u), align_bytes=64),
-                    "codes": sb.tile([P, W], U32, name="%s%d_codes" % (name, first + u), align_bytes=64),
-                    "scales": sb.tile([P, W], U8, name="%s%d_scales" % (name, first + u), align_bytes=64),
-                }
-                for u in range(count)
-            ]
+        def load_operand(name, src):
+            width = src.shape[2]
+            raw = sb.tile([P, PACK, width], F32, name=name + "_raw")
+            nc.sync.dma_start(out=raw[:], in_=src.rearrange("g (p j) n -> (g p) j n", j=PACK))
+            return {
+                "raw": raw,
+                "bf": sb.tile([P, width, PACK], BF16, name=name + "_bf", align_bytes=64),
+                "codes": sb.tile([P, width], U32, name=name + "_codes", align_bytes=64),
+                "scales": sb.tile([P, width], U8, name=name + "_scales", align_bytes=64),
+            }
 
         def load_old(first, count):
             raw = sb.tile([P, G, count * W], F32, name="old%d" % first)
             nc.sync.dma_start(out=raw[:], in_=old[:, :, first * W : (first + count) * W].rearrange("g m n -> m g n"))
             return [raw[:, :, cols[u]] for u in range(count)]
 
-        def interleave(copy, op, n=slice(0, W)):
+        def interleave(copy, op, n=slice(None)):
             copy(
                 out=op["bf"][:, n, :].rearrange("p (c i) j -> p c j i", i=RUN),
                 in_=op["raw"][:, :, n].rearrange("p j (c i) -> p c j i", i=RUN),
             )
 
-        def quantize(op):
+        def quantize(op, n=slice(None)):
             nc.vector.quantize_mx(
-                out=op["codes"][:].bitcast(FP8X4),
-                scales=op["scales"][:],
-                in_=op["bf"][:].rearrange("p n j -> p (n j)"),
+                out=op["codes"][:, n].bitcast(FP8X4),
+                scales=op["scales"][:, n],
+                in_=op["bf"][:, n, :].rearrange("p n j -> p (n j)"),
             )
 
         def product(target, weights, moving, g):
             rows = slice(ROWS * g, ROWS * (g + 1))
-            nc.tensor.matmul_mx(
-                out=target,
-                lhsT=weights["codes"][rows, :].bitcast(FP8X4),
-                lhsT_scale=weights["scales"][rows, :],
-                rhs=moving["codes"][rows, :].bitcast(FP8X4),
-                rhs_scale=moving["scales"][rows, :],
-                start=True,
-                stop=True,
-            )
+            for n0 in range(0, W, N_CALL):
+                n = slice(n0, n0 + N_CALL)
+                nc.tensor.matmul_mx(
+                    out=target[:, n],
+                    lhsT=weights["codes"][rows, :].bitcast(FP8X4),
+                    lhsT_scale=weights["scales"][rows, :],
+                    rhs=moving["codes"][rows, n].bitcast(FP8X4),
+                    rhs_scale=moving["scales"][rows, n],
+                    start=True,
+                    stop=True,
+                )
 
         on_vector, on_scalar = nc.vector.tensor_copy, nc.scalar.copy
 
@@ -95,18 +93,15 @@ def tile_rows_bsphere_kernel(tc, x, w1, w2, ra, wo, dy, old, out):
         nc.scalar.activation(out=warm[:], in_=one[:], func=ACT.Abs_reciprocal_sqrt)
         ra_col = [ra_cols[:, 32 * g : 32 * g + 1] for g in range(G)]
 
-        xs = load_operand("x", x, 0, 1)
-        (w1q,) = load_operand("w1", w1, 0, 1)
-        (w2q,) = load_operand("w2", w2, 0, 1)
-        xs = xs + load_operand("x", x, 1, 1)
-        (woq,) = load_operand("wo", wo, 0, 1)
-        dys = load_operand("dy", dy, 0, 1)
-        xs = xs + load_operand("x", x, 2, 1)
-        dys = dys + load_operand("dy", dy, 1, 1)
+        xs = [load_operand("x0", x[:, :, cols[0]])]
+        w1q = load_operand("w1", w1)
+        w2q = load_operand("w2", w2)
+        woq = load_operand("wo", wo)
+        dys = [load_operand("dy0", dy[:, :, cols[0]])]
+        xs.append(load_operand("x1", x[:, :, cols[1]]))
         olds = load_old(0, 1)
-        xs = xs + load_operand("x", x, 3, 1)
-        dys = dys + load_operand("dy", dy, 2, 2)
-        olds = olds + load_old(1, 3)
+        dys.append(load_operand("dy1", dy[:, :, cols[1]]))
+        olds = olds + load_old(1, 1)
 
         def planes(name, per=1):
             return [sb.tile([P, G, per * W], F32, name="%s%d" % (name, c)) for c in range(UNITS)]
@@ -114,13 +109,13 @@ def tile_rows_bsphere_kernel(tc, x, w1, w2, ra, wo, dy, old, out):
         sq, s, r, r2, t, q, y, o = planes("sq", 2), planes("s"), planes("r"), planes("rr"), planes("t"), planes("q"), planes("y"), planes("o")
         lo, hi, both = slice(0, 2), slice(2, 4), slice(0, 4)
 
-        def z_products(c):
-            for g in range(G):
+        def z_products(c, gs=both):
+            for g in range(gs.start, gs.stop):
                 product(z_bank[g][:, :W], w1q, xs[c], g)
                 product(z_bank[g][:, W : 2 * W], w2q, xs[c], g)
 
-        def c_products(c):
-            for g in range(G):
+        def c_products(c, gs=both):
+            for g in range(gs.start, gs.stop):
                 product(c_bank[g][:, cols[c]], woq, dys[c], g)
 
         def squares(c, gs=both):
@@ -156,75 +151,74 @@ def tile_rows_bsphere_kernel(tc, x, w1, w2, ra, wo, dy, old, out):
         def store(c, gs=both):
             nc.sync.dma_start(out=out[gs, :, cols[c]].rearrange("g m n -> m g n"), in_=o[c][:, gs, :])
 
-        interleave(on_vector, xs[0])
-        interleave(on_vector, w1q)
+        g2, g3 = slice(2, 3), slice(3, 4)
+        interleave(on_vector, xs[0], slice(0, 160))
+        interleave(on_scalar, xs[0], slice(160, 256))
+        interleave(on_vector, w1q, slice(0, 80))
+        interleave(on_scalar, w1q, slice(80, 128))
         quantize(xs[0])
-        interleave(on_scalar, w2q, slice(80, 128))
-        interleave(on_vector, w2q, slice(0, 80))
         quantize(w1q)
-        for g in range(G):
-            product(c_bank[g][:, :W], w1q, xs[0], g)
+        interleave(on_vector, w2q, slice(0, 80))
+        interleave(on_scalar, w2q, slice(80, 128))
         quantize(w2q)
-        for g in range(G):
-            product(z_bank[g][:, :W], w2q, xs[0], g)
-        for g in range(G):
-            nc.scalar.activation(out=sq[0][:, g, :W], in_=c_bank[g][:, :W], func=ACT.Square)
-        for g in range(G):
-            nc.scalar.activation(out=sq[0][:, g, W:], in_=z_bank[g][:, :W], func=ACT.Square)
-        interleave(on_vector, xs[1])
-        nc.vector.transpose(out=ra_cols[:], in_=ra_rows[:])
-        quantize(xs[1])
-        z_products(1)
-        squares(1)
+        for gs in (lo, hi):
+            for g in range(gs.start, gs.stop):
+                product(c_bank[g][:, :W], w1q, xs[0], g)
+            for g in range(gs.start, gs.stop):
+                product(z_bank[g][:, :W], w2q, xs[0], g)
+            for g in range(gs.start, gs.stop):
+                nc.scalar.activation(out=sq[0][:, g, :W], in_=c_bank[g][:, :W], func=ACT.Square)
+            for g in range(gs.start, gs.stop):
+                nc.scalar.activation(out=sq[0][:, g, W:], in_=z_bank[g][:, :W], func=ACT.Square)
         interleave(on_vector, woq)
+        nc.vector.transpose(out=ra_cols[:], in_=ra_rows[:])
         quantize(woq)
         interleave(on_vector, dys[0])
         sums(0, lo)
         quantize(dys[0])
         c_products(0)
+        interleave(on_vector, xs[1], slice(0, XS))
+        interleave(on_scalar, xs[1], slice(XS, 256))
         sums(0, hi)
-
-        interleave(on_vector, xs[2])
-        for c in range(UNITS):
-            first, last = c == 0, c + 1 == UNITS
-            roots(c)
-            if not last:
-                interleave(on_scalar, dys[c + 1])
-            if last:
-                inverses(c, lo)
-                inverses(c, hi)
-            else:
-                inverses(c)
-            if c + 3 < UNITS:
-                interleave(on_scalar, xs[c + 3])
-            numerators(c, lo)
-            if first:
-                quantize(xs[2])
-                z_products(2)
-            numerators(c, hi)
-            if c + 2 < UNITS:
-                squares(c + 2)
-            if first:
-                sums(1)
-            else:
-                add_old(c - 1)
-                store(c - 1)
-            if not last:
-                by_root(c)
-                quantize(dys[c + 1])
-                c_products(c + 1)
-                if not first:
-                    sums(c + 1)
-                by_inverse(c)
-                if first:
-                    quantize(xs[3])
-                    z_products(3)
-        c = UNITS - 1
-        by_root(c, lo)
-        by_root(c, hi)
-        by_inverse(c, lo)
-        by_inverse(c, hi)
-        add_old(c, lo)
-        store(c, lo)
-        add_old(c, hi)
-        store(c, hi)
+        quantize(xs[1])
+        z_products(1)
+        roots(0)
+        inverses(0, lo)
+        inverses(0, hi)
+        interleave(on_scalar, dys[1])
+        squares(1)
+        numerators(0)
+        by_root(0, lo)
+        by_root(0, hi)
+        by_inverse(0, lo)
+        by_inverse(0, hi)
+        add_old(0, lo)
+        store(0, lo)
+        quantize(dys[1])
+        c_products(1)
+        add_old(0, hi)
+        store(0, hi)
+        sums(1, lo)
+        sums(1, g2)
+        numerators(1, lo)
+        sums(1, g3)
+        roots(1, lo)
+        roots(1, g2)
+        inverses(1, lo)
+        roots(1, g3)
+        inverses(1, g2)
+        inverses(1, g3)
+        numerators(1, g2)
+        by_root(1, lo)
+        numerators(1, g3)
+        by_root(1, g2)
+        by_inverse(1, lo)
+        by_root(1, g3)
+        add_old(1, lo)
+        store(1, lo)
+        by_inverse(1, g2)
+        by_inverse(1, g3)
+        add_old(1, g2)
+        store(1, g2)
+        add_old(1, g3)
+        store(1, g3)

@@ -20,7 +20,7 @@ N_CALL = 128
 RUN = 4
 W = 256
 UNITS = N // W
-XS = 128
+XS = 96
 
 
 def tile_rows_bsphere_kernel(tc, x, w1, w2, ra, wo, dy, old, out):
@@ -46,10 +46,10 @@ def tile_rows_bsphere_kernel(tc, x, w1, w2, ra, wo, dy, old, out):
                 "scales": sb.tile([P, width], U8, name=name + "_scales", align_bytes=64),
             }
 
-        def load_old(first, count):
-            raw = sb.tile([P, G, count * W], F32, name="old%d" % first)
-            nc.sync.dma_start(out=raw[:], in_=old[:, :, first * W : (first + count) * W].rearrange("g m n -> m g n"))
-            return [raw[:, :, cols[u]] for u in range(count)]
+        def load_old(gs):
+            raw = sb.tile([P, gs.stop - gs.start, N], F32, name="old%d" % gs.start)
+            nc.sync.dma_start(out=raw[:], in_=old[gs].rearrange("g m n -> m g n"))
+            return raw
 
         def interleave(copy, op, n=slice(None)):
             copy(
@@ -96,12 +96,11 @@ def tile_rows_bsphere_kernel(tc, x, w1, w2, ra, wo, dy, old, out):
         xs = [load_operand("x0", x[:, :, cols[0]])]
         w1q = load_operand("w1", w1)
         w2q = load_operand("w2", w2)
-        woq = load_operand("wo", wo)
         dys = [load_operand("dy0", dy[:, :, cols[0]])]
+        woq = load_operand("wo", wo)
         xs.append(load_operand("x1", x[:, :, cols[1]]))
-        olds = load_old(0, 1)
         dys.append(load_operand("dy1", dy[:, :, cols[1]]))
-        olds = olds + load_old(1, 1)
+        olds = [load_old(slice(0, 2)), load_old(slice(2, 4))]
 
         def planes(name, per=1):
             return [sb.tile([P, G, per * W], F32, name="%s%d" % (name, c)) for c in range(UNITS)]
@@ -145,11 +144,14 @@ def tile_rows_bsphere_kernel(tc, x, w1, w2, ra, wo, dy, old, out):
         def by_inverse(c, gs=both):
             nc.vector.tensor_tensor(out=y[c][:, gs, :], in0=q[c][:, gs, :], in1=r2[c][:, gs, :], op=ALU.mult)
 
-        def add_old(c, gs=both):
-            nc.vector.tensor_tensor(out=o[c][:, gs, :], in0=y[c][:, gs, :], in1=olds[c][:, gs, :], op=ALU.add)
+        def add_old(c, gs, n=slice(0, W), engine=nc.vector):
+            first = gs.start % 2
+            src = olds[gs.start // 2][:, first : first + gs.stop - gs.start, c * W + n.start : c * W + n.stop]
+            engine.tensor_tensor(out=o[c][:, gs, n], in0=y[c][:, gs, n], in1=src, op=ALU.add)
 
-        def store(c, gs=both):
-            nc.sync.dma_start(out=out[gs, :, cols[c]].rearrange("g m n -> m g n"), in_=o[c][:, gs, :])
+        def store(c, gs, n=slice(0, W)):
+            dst = out[gs, :, c * W + n.start : c * W + n.stop]
+            nc.sync.dma_start(out=dst.rearrange("g m n -> m g n"), in_=o[c][:, gs, n])
 
         g2, g3 = slice(2, 3), slice(3, 4)
         interleave(on_vector, xs[0], slice(0, 160))
@@ -161,7 +163,7 @@ def tile_rows_bsphere_kernel(tc, x, w1, w2, ra, wo, dy, old, out):
         interleave(on_vector, w2q, slice(0, 80))
         interleave(on_scalar, w2q, slice(80, 128))
         quantize(w2q)
-        for gs in (lo, hi):
+        for gs in (lo, g2, g3):
             for g in range(gs.start, gs.stop):
                 product(c_bank[g][:, :W], w1q, xs[0], g)
             for g in range(gs.start, gs.stop):
@@ -170,16 +172,18 @@ def tile_rows_bsphere_kernel(tc, x, w1, w2, ra, wo, dy, old, out):
                 nc.scalar.activation(out=sq[0][:, g, :W], in_=c_bank[g][:, :W], func=ACT.Square)
             for g in range(gs.start, gs.stop):
                 nc.scalar.activation(out=sq[0][:, g, W:], in_=z_bank[g][:, :W], func=ACT.Square)
-        interleave(on_vector, woq)
         nc.vector.transpose(out=ra_cols[:], in_=ra_rows[:])
-        quantize(woq)
         interleave(on_vector, dys[0])
-        sums(0, lo)
+        interleave(on_vector, woq)
         quantize(dys[0])
+        quantize(woq)
         c_products(0)
+        sums(0, lo)
         interleave(on_vector, xs[1], slice(0, XS))
         interleave(on_scalar, xs[1], slice(XS, 256))
-        sums(0, hi)
+        sums(0, g2)
+        numerators(0, lo)
+        sums(0, g3)
         quantize(xs[1])
         z_products(1)
         roots(0)
@@ -187,7 +191,7 @@ def tile_rows_bsphere_kernel(tc, x, w1, w2, ra, wo, dy, old, out):
         inverses(0, hi)
         interleave(on_scalar, dys[1])
         squares(1)
-        numerators(0)
+        numerators(0, hi)
         by_root(0, lo)
         by_root(0, hi)
         by_inverse(0, lo)

from contextlib import ExitStack

import concourse.mybir as mybir

G, D, M, N = 4, 128, 128, 512
FLOPS = 3 * 2 * G * D * M * N

F32 = mybir.dt.float32
BF16 = mybir.dt.bfloat16
U32 = mybir.dt.uint32
U8 = mybir.dt.uint8
FP8X4 = mybir.dt.float8_e4m3fn_x4
ACT = mybir.ActivationFunctionType
ALU = mybir.AluOpType

P = 128
PACK = 4
ROWS = D // PACK
N_CALL = 128
RUN = 4
W = 256
UNITS = N // W
XS = 96


def tile_rows_bsphere_kernel(tc, x, w1, w2, ra, wo, dy, old, out):
    nc = tc.nc
    cols = [slice(W * c, W * (c + 1)) for c in range(UNITS)]

    with ExitStack() as ctx:
        sb = ctx.enter_context(tc.tile_pool(name="sb", bufs=1))
        ps = ctx.enter_context(tc.psum_pool(name="ps", bufs=1))
        ctx.enter_context(tc.manual_schedule())

        z_bank = [ps.tile([P, N], F32, name="z%d" % g) for g in range(G)]
        c_bank = [ps.tile([P, N], F32, name="c%d" % g) for g in range(G)]

        def load_operand(name, src):
            width = src.shape[2]
            raw = sb.tile([P, PACK, width], F32, name=name + "_raw")
            nc.sync.dma_start(out=raw[:], in_=src.rearrange("g (p j) n -> (g p) j n", j=PACK))
            return {
                "raw": raw,
                "bf": sb.tile([P, width, PACK], BF16, name=name + "_bf", align_bytes=64),
                "codes": sb.tile([P, width], U32, name=name + "_codes", align_bytes=64),
                "scales": sb.tile([P, width], U8, name=name + "_scales", align_bytes=64),
            }

        def load_old(gs):
            raw = sb.tile([P, gs.stop - gs.start, N], F32, name="old%d" % gs.start)
            nc.sync.dma_start(out=raw[:], in_=old[gs].rearrange("g m n -> m g n"))
            return raw

        def interleave(copy, op, n=slice(None)):
            copy(
                out=op["bf"][:, n, :].rearrange("p (c i) j -> p c j i", i=RUN),
                in_=op["raw"][:, :, n].rearrange("p j (c i) -> p c j i", i=RUN),
            )

        def quantize(op, n=slice(None)):
            nc.vector.quantize_mx(
                out=op["codes"][:, n].bitcast(FP8X4),
                scales=op["scales"][:, n],
                in_=op["bf"][:, n, :].rearrange("p n j -> p (n j)"),
            )

        def product(target, weights, moving, g):
            rows = slice(ROWS * g, ROWS * (g + 1))
            for n0 in range(0, W, N_CALL):
                n = slice(n0, n0 + N_CALL)
                nc.tensor.matmul_mx(
                    out=target[:, n],
                    lhsT=weights["codes"][rows, :].bitcast(FP8X4),
                    lhsT_scale=weights["scales"][rows, :],
                    rhs=moving["codes"][rows, n].bitcast(FP8X4),
                    rhs_scale=moving["scales"][rows, n],
                    start=True,
                    stop=True,
                )

        on_vector, on_scalar = nc.vector.tensor_copy, nc.scalar.copy

        ra_rows = sb.tile([P, P], F32, name="ra_rows", align_bytes=64)
        ra_cols = sb.tile([P, P], F32, name="ra_cols", align_bytes=64)
        one = sb.tile([P, 8], F32, name="one")
        warm = sb.tile([P, 8], F32, name="warm")
        nc.vector.memset(ra_rows[:], 0.0)
        nc.vector.memset(one[:], 1.0)
        nc.scalar.dma_start(
            out=ra_rows[0:P:32, :].rearrange("a (g i) -> a g i", g=G),
            in_=ra.rearrange("g (a i) o -> a g (i o)", i=32),
        )
        nc.scalar.activation(out=warm[:], in_=one[:], func=ACT.Abs_reciprocal_sqrt)
        ra_col = [ra_cols[:, 32 * g : 32 * g + 1] for g in range(G)]

        xs = [load_operand("x0", x[:, :, cols[0]])]
        w1q = load_operand("w1", w1)
        w2q = load_operand("w2", w2)
        dys = [load_operand("dy0", dy[:, :, cols[0]])]
        woq = load_operand("wo", wo)
        xs.append(load_operand("x1", x[:, :, cols[1]]))
        dys.append(load_operand("dy1", dy[:, :, cols[1]]))
        olds = [load_old(slice(0, 2)), load_old(slice(2, 4))]

        def planes(name, per=1):
            return [sb.tile([P, G, per * W], F32, name="%s%d" % (name, c)) for c in range(UNITS)]

        sq, s, r, r2, t, q, y, o = planes("sq", 2), planes("s"), planes("r"), planes("rr"), planes("t"), planes("q"), planes("y"), planes("o")
        lo, hi, both = slice(0, 2), slice(2, 4), slice(0, 4)

        def z_products(c, gs=both):
            for g in range(gs.start, gs.stop):
                product(z_bank[g][:, :W], w1q, xs[c], g)
                product(z_bank[g][:, W : 2 * W], w2q, xs[c], g)

        def c_products(c, gs=both):
            for g in range(gs.start, gs.stop):
                product(c_bank[g][:, cols[c]], woq, dys[c], g)

        def squares(c, gs=both):
            for g in range(gs.start, gs.stop):
                nc.scalar.activation(out=sq[c][:, g, :], in_=z_bank[g][:, : 2 * W], func=ACT.Square)

        def sums(c, gs=both):
            nc.vector.tensor_tensor(out=s[c][:, gs, :], in0=sq[c][:, gs, :W], in1=sq[c][:, gs, W:], op=ALU.add)

        def roots(c, gs=both):
            for g in range(gs.start, gs.stop):
                nc.scalar.activation(out=r[c][:, g, :], in_=s[c][:, g, :], func=ACT.Abs_reciprocal_sqrt, bias=ra_col[g])

        def inverses(c, gs=both):
            nc.scalar.activation(out=r2[c][:, gs, :], in_=r[c][:, gs, :], func=ACT.Square)

        def numerators(c, gs=both):
            for g in range(gs.start, gs.stop):
                nc.vector.scalar_tensor_tensor(
                    out=t[c][:, g, :], in0=sq[c][:, g, W:], scalar=ra_col[g], in1=c_bank[g][:, cols[c]],
                    op0=ALU.add, op1=ALU.mult,
                )

        def by_root(c, gs=both):
            nc.vector.tensor_tensor(out=q[c][:, gs, :], in0=t[c][:, gs, :], in1=r[c][:, gs, :], op=ALU.mult)

        def by_inverse(c, gs=both):
            nc.vector.tensor_tensor(out=y[c][:, gs, :], in0=q[c][:, gs, :], in1=r2[c][:, gs, :], op=ALU.mult)

        def add_old(c, gs, n=slice(0, W), engine=nc.vector):
            first = gs.start % 2
            src = olds[gs.start // 2][:, first : first + gs.stop - gs.start, c * W + n.start : c * W + n.stop]
            engine.tensor_tensor(out=o[c][:, gs, n], in0=y[c][:, gs, n], in1=src, op=ALU.add)

        def store(c, gs, n=slice(0, W)):
            dst = out[gs, :, c * W + n.start : c * W + n.stop]
            nc.sync.dma_start(out=dst.rearrange("g m n -> m g n"), in_=o[c][:, gs, n])

        g2, g3 = slice(2, 3), slice(3, 4)
        interleave(on_vector, xs[0], slice(0, 160))
        interleave(on_scalar, xs[0], slice(160, 256))
        interleave(on_vector, w1q, slice(0, 80))
        interleave(on_scalar, w1q, slice(80, 128))
        quantize(xs[0])
        quantize(w1q)
        interleave(on_vector, w2q, slice(0, 80))
        interleave(on_scalar, w2q, slice(80, 128))
        quantize(w2q)
        for gs in (lo, g2, g3):
            for g in range(gs.start, gs.stop):
                product(c_bank[g][:, :W], w1q, xs[0], g)
            for g in range(gs.start, gs.stop):
                product(z_bank[g][:, :W], w2q, xs[0], g)
            for g in range(gs.start, gs.stop):
                nc.scalar.activation(out=sq[0][:, g, :W], in_=c_bank[g][:, :W], func=ACT.Square)
            for g in range(gs.start, gs.stop):
                nc.scalar.activation(out=sq[0][:, g, W:], in_=z_bank[g][:, :W], func=ACT.Square)
        nc.vector.transpose(out=ra_cols[:], in_=ra_rows[:])
        interleave(on_vector, dys[0])
        interleave(on_vector, woq)
        quantize(dys[0])
        quantize(woq)
        c_products(0)
        sums(0, lo)
        interleave(on_vector, xs[1], slice(0, XS))
        interleave(on_scalar, xs[1], slice(XS, 256))
        sums(0, g2)
        numerators(0, lo)
        sums(0, g3)
        quantize(xs[1])
        z_products(1)
        roots(0)
        inverses(0, lo)
        inverses(0, hi)
        interleave(on_scalar, dys[1])
        squares(1)
        numerators(0, hi)
        by_root(0, lo)
        by_root(0, hi)
        by_inverse(0, lo)
        by_inverse(0, hi)
        add_old(0, lo)
        store(0, lo)
        quantize(dys[1])
        c_products(1)
        add_old(0, hi)
        store(0, hi)
        sums(1, lo)
        sums(1, g2)
        numerators(1, lo)
        sums(1, g3)
        roots(1, lo)
        roots(1, g2)
        inverses(1, lo)
        roots(1, g3)
        inverses(1, g2)
        inverses(1, g3)
        numerators(1, g2)
        by_root(1, lo)
        numerators(1, g3)
        by_root(1, g2)
        by_inverse(1, lo)
        by_root(1, g3)
        add_old(1, lo)
        store(1, lo)
        by_inverse(1, g2)
        by_inverse(1, g3)
        add_old(1, g2)
        store(1, g2)
        add_old(1, g3)
        store(1, g3)
